import numpy as np
import ml_dtypes


def mxq(x, axis, fmt="e4m3"):
    dtype, down = {"e4m3": (ml_dtypes.float8_e4m3fn, 7), "e5m2": (ml_dtypes.float8_e5m2, 14)}[fmt]
    v = np.moveaxis(np.asarray(x, np.float32).astype(ml_dtypes.bfloat16).astype(np.float64), axis, -1)
    blocks = v.reshape(v.shape[:-1] + (-1, 32))
    amax = np.abs(blocks).max(-1, keepdims=True)
    byte = np.maximum(np.where(amax > 0, np.frexp(amax)[1] - 1 + 127, 0) - down, 1)
    scale = np.exp2(byte - 127.0)
    codes = (blocks / scale).astype(np.float32).astype(dtype).astype(np.float64)
    return np.moveaxis((codes * scale).reshape(v.shape), -1, axis)


WIDE = False


def mx_kscale(k):
    if not WIDE:
        return np.ones(k)
    levels = np.array([30, -30])
    if k % 512:
        return np.exp2(np.random.permutation(np.resize(levels, k // 32))).repeat(32)
    a = np.empty((k // 512, 16))
    for p in range(k // 512):
        a[p, :8] = np.random.permutation(np.resize(levels, 8))
        for g in range(8):
            far = levels[np.abs(levels - a[p, g]) >= 10]
            a[p, g + 8] = far[np.random.randint(len(far))]
    return np.exp2(a.ravel()).repeat(32)


def f64(x):
    return np.asarray(x).astype(np.float64)


def striped(idx):
    return np.tile(np.asarray(idx).reshape(-1, 16).T, (8, 1)).astype(np.uint16)


def unstriped(offs):
    return offs[:16].T.reshape(-1).astype(np.int64)


E2M1 = np.array([0.0, 0.5, 1.0, 1.5, 2.0, 3.0, 4.0, 6.0, -0.0, -0.5, -1.0, -1.5, -2.0, -3.0, -4.0, -6.0])


def pack_weight(w, fmt):
    k, n = w.shape
    w = f64(np.asarray(w, np.float32).astype(ml_dtypes.bfloat16)).reshape(k // 32, 32, n)
    amax = np.abs(w).max(1)
    if fmt in ("e4m3", "e5m2"):
        byte = np.frexp(amax)[1] - 1 + 127 - (7 if fmt == "e4m3" else 14)
    else:
        mant, ex = np.frexp(amax / 6.0)
        byte = np.where(mant > 0.5, ex, ex - 1) + 127
    byte = np.clip(np.where(amax > 0, byte, 1), 1, 254)
    scaled = (w * np.exp2(127.0 - byte)[:, None, :]).reshape(k, n).astype(np.float32)
    by_word = np.ascontiguousarray(scaled.reshape(k // 512, 128, 4, n).transpose(0, 1, 3, 2))
    if fmt in ("e4m3", "e5m2"):
        words = by_word.astype(ml_dtypes.float8_e4m3fn if fmt == "e4m3" else ml_dtypes.float8_e5m2).view(np.uint8)
    else:
        c = by_word.astype(ml_dtypes.float4_e2m1fn).view(np.uint8) & 0xF
        words = (c[..., 0::2] | (c[..., 1::2] << 4)).reshape(k // 512, 128, 2 * n)
    return np.ascontiguousarray(words), np.ascontiguousarray(byte.astype(np.uint8).reshape(k // 512, 16, n))


def unpack_weight(words, scales, fmt):
    g, _, n = scales.shape
    words = np.ascontiguousarray(words).reshape(g, 128, n, -1)
    if fmt in ("e4m3", "e5m2"):
        vals = words.view(ml_dtypes.float8_e4m3fn if fmt == "e4m3" else ml_dtypes.float8_e5m2).astype(np.float64)
    else:
        nib = np.empty((g, 128, n, 4), np.uint8)
        nib[..., 0::2] = words & 0xF
        nib[..., 1::2] = words >> 4
        vals = E2M1[nib]
    vals = vals * np.repeat(np.exp2(scales.astype(np.float64) - 127.0), 8, axis=1)[..., None]
    return vals.transpose(0, 1, 3, 2).reshape(g * 512, n)


K, T, Z, J, R, C, O, N = 512, 1024, 1024, 256, 512, 512, 256, 256


def setup_inputs():
    n = np.random.standard_normal
    idx = np.random.permutation(T)[:J]
    idx2 = np.random.permutation(Z)[:J]
    idx3 = np.random.permutation(C)[:J]
    idx4 = np.random.permutation(C)[:J]
    idx5 = np.random.permutation(C)[:O]
    idx6 = np.random.permutation(C)[:O]
    fk = mx_kscale(K)
    fr = mx_kscale(R)
    xtp = pack_weight(n((K, T)) / fk[:, None], "e2m1")
    xop = pack_weight(n((K, Z)) / fk[:, None], "e5m2")
    wp = pack_weight(n((K, R)) * 1 / np.sqrt(K) * fk[:, None] * fr, "e5m2")
    w2p = pack_weight(n((K, R)) * 1 / np.sqrt(K) * fk[:, None] * fr, "e4m3")
    wbp = pack_weight(n((R, N)) * 1 / np.sqrt(R) / fr[:, None], "e4m3")
    return {
        "xt_words": xtp[0],
        "xt_scales": xtp[1],
        "xo_words": xop[0],
        "xo_scales": xop[1],
        "w_words": wp[0],
        "w_scales": wp[1],
        "w2_words": w2p[0],
        "w2_scales": w2p[1],
        "wb_words": wbp[0],
        "wb_scales": wbp[1],
        "offs": striped(idx),
        "offs2": striped(idx2),
        "offs3": striped(idx3),
        "offs4": striped(idx4),
        "offs5": striped(idx5),
        "offs6": striped(idx6),
    }


def reference(xt_words, xt_scales, xo_words, xo_scales, w_words, w_scales, w2_words, w2_scales, wb_words, wb_scales, offs, offs2, offs3, offs4, offs5, offs6):
    idx = unstriped(offs)
    idx2 = unstriped(offs2)
    idx3 = unstriped(offs3)
    idx4 = unstriped(offs4)
    idx5 = unstriped(offs5)
    idx6 = unstriped(offs6)
    xtu = unpack_weight(xt_words, xt_scales, "e2m1")
    xou = unpack_weight(xo_words, xo_scales, "e5m2")
    wu = unpack_weight(w_words, w_scales, "e5m2")
    w2u = unpack_weight(w2_words, w2_scales, "e4m3")
    wbu = unpack_weight(wb_words, wb_scales, "e4m3")
    xtidxg = xtu[:, idx]
    xoidx2g = xou[:, idx2]
    a = wu.T @ xtidxg + w2u.T @ xoidx2g
    b = w2u.T @ xtidxg + wu.T @ xoidx2g
    pw = np.zeros((R, C))
    pw[:, idx3] = a
    pv = np.zeros((R, C))
    pv[:, idx4] = b
    hid = np.abs(pw[:, idx5] - pv[:, idx6])
    hidq = mxq(hid, 0, "e5m2")
    y = wbu.T @ hidq
    return y

@@ -1,0 +1,166 @@
+from contextlib import ExitStack
+
+import concourse.mybir as mybir
+
+K, T, Z, J, R, C, O, N = 512, 1024, 1024, 256, 512, 512, 256, 256
+FLOPS = 2 * (4 * K * R * J + R * N * O)
+
+F32 = mybir.dt.float32
+BF16 = mybir.dt.bfloat16
+I32 = mybir.dt.int32
+U32 = mybir.dt.uint32
+U16 = mybir.dt.uint16
+U8 = mybir.dt.uint8
+E4M3 = mybir.dt.float8_e4m3fn_x4
+E5M2 = mybir.dt.float8_e5m2_x4
+E2M1 = mybir.dt.float4_e2m1fn_x4
+ACT = mybir.ActivationFunctionType
+ALU = mybir.AluOpType
+
+P = 128
+PACK = 4
+
+
+def tile_list_crossed_twoboards_one_plain_kernel(
+    tc, xt_words, xt_scales, xo_words, xo_scales, w_words, w_scales, w2_words, w2_scales,
+    wb_words, wb_scales, offs, offs2, offs3, offs4, offs5, offs6, out,
+):
+    nc = tc.nc
+    with ExitStack() as ctx:
+        lists = ctx.enter_context(tc.tile_pool(name="lists", bufs=1))
+        keep = ctx.enter_context(tc.tile_pool(name="keep", bufs=1))
+        psum = ctx.enter_context(tc.psum_pool(name="psum", bufs=8))
+
+        def load_list(name, src):
+            tile = lists.tile([P, J // 16], U16, name=name)
+            nc.sync.dma_start(tile[:], src)
+            return tile
+
+        def load_words(name, src, cols, dtype, queue):
+            tile = keep.tile([P, cols], dtype, name=name, align_bytes=64)
+            queue.dma_start(tile[:].bitcast(I32), src.bitcast(I32))
+            return tile
+
+        def load_plane(name, src, cols, queue):
+            tile = keep.tile([P, cols], U8, name=name, align_bytes=64)
+            nc.vector.memset(tile[:].bitcast(I32), 0)
+            rows = src[0].bitcast(I32)
+            for q in range(4):
+                queue.dma_start(tile[32 * q : 32 * q + 4, :].bitcast(I32), rows[4 * q : 4 * q + 4, :])
+            return tile
+
+        def flat(words):
+            return words[0].rearrange("p c t -> p (c t)")
+
+        idx = load_list("idx", offs)
+        xt_w = load_words("xt_w", xt_words[0], T, U16, nc.sync)
+        idx2 = load_list("idx2", offs2)
+        xo_w = load_words("xo_w", flat(xo_words), Z, U32, nc.sync)
+        xt_s = load_plane("xt_s", xt_scales, T, nc.sync)
+        w_w = load_words("w_w", flat(w_words), R, U32, nc.sync)
+        w2_w = load_words("w2_w", flat(w2_words), R, U32, nc.sync)
+        xo_s = load_plane("xo_s", xo_scales, Z, nc.sync)
+        w_s = load_plane("w_s", w_scales, R, nc.sync)
+        w2_s = load_plane("w2_s", w2_scales, R, nc.sync)
+        idx3 = load_list("idx3", offs3)
+        idx4 = load_list("idx4", offs4)
+        idx5 = load_list("idx5", offs5)
+        idx6 = load_list("idx6", offs6)
+        wb_w = load_words("wb_w", flat(wb_words), N, U32, nc.sync)
+        wb_s = load_plane("wb_s", wb_scales, N, nc.sync)
+
+        boards_w = [keep.tile([P, C], F32, name="pw%d" % t) for t in range(PACK)]
+        boards_v = [keep.tile([P, C], F32, name="pv%d" % t) for t in range(PACK)]
+        for t in range(PACK):
+            nc.vector.memset(boards_w[t][:], 0.0)
+            nc.vector.memset(boards_v[t][:], 0.0)
+
+        def pick(name, window, offsets, dtype):
+            tile = keep.tile([P, J], dtype, name=name, align_bytes=64)
+            nc.vector.tensor_copy(tile[:], window[:].indirect(offsets[:]))
+            return tile
+
+        xt_wg = pick("xt_wg", xt_w, idx, U16)
+        xt_sg = pick("xt_sg", xt_s, idx, U8)
+        xo_wg = pick("xo_wg", xo_w, idx2, U32)
+        xo_sg = pick("xo_sg", xo_s, idx2, U8)
+
+        def deal(name, src, dtype, run, copy):
+            tile = keep.tile([P, R], dtype, name=name, align_bytes=64)
+            copy(
+                tile[:].rearrange("p (t c i) -> p c t i", t=PACK, i=run),
+                src[:].rearrange("p (c i t) -> p c t i", t=PACK, i=run),
+            )
+            return tile
+
+        w_wd = deal("w_wd", w_w, U32, 4, nc.scalar.copy)
+        w_sd = deal("w_sd", w_s, U8, 16, nc.vector.tensor_copy)
+        w2_wd = deal("w2_wd", w2_w, U32, 4, nc.scalar.copy)
+        w2_sd = deal("w2_sd", w2_s, U8, 16, nc.vector.tensor_copy)
+
+        first = (w_wd, w_sd, E5M2)
+        second = (w2_wd, w2_sd, E4M3)
+        tokens = (xt_wg, xt_sg, E2M1)
+        notes = (xo_wg, xo_sg, E5M2)
+
+        def product(acc, weight, cols, moving, start, stop):
+            nc.tensor.matmul_mx(
+                out=acc,
+                lhsT=weight[0][:, cols].bitcast(weight[2]),
+                lhsT_scale=weight[1][:, cols],
+                rhs=moving[0][:].bitcast(moving[2]),
+                rhs_scale=moving[1][:],
+                start=start,
+                stop=stop,
+            )
+
+        sums = []
+        for t in range(PACK):
+            cols = slice(t * P, (t + 1) * P)
+            a_ps = psum.tile([P, J], F32, tag="bank", name="a_ps")
+            product(a_ps[:], first, cols, tokens, True, False)
+            product(a_ps[:], second, cols, notes, False, True)
+            b_ps = psum.tile([P, J], F32, tag="bank", name="b_ps")
+            product(b_ps[:], second, cols, tokens, True, False)
+            product(b_ps[:], first, cols, notes, False, True)
+            sums.append((a_ps, b_ps))
+
+        halves = [slice(h * P, (h + 1) * P) for h in range(O // P)]
+        diffs = [keep.tile([P, PACK, P], F32, name="diff%d" % h) for h in range(O // P)]
+        a_sb = [keep.tile([P, J], F32, name="a_sb%d" % t) for t in range(PACK)]
+        b_sb = [keep.tile([P, J], F32, name="b_sb%d" % t) for t in range(PACK)]
+        read_w = [keep.tile([P, O], F32, name="read_w%d" % t) for t in range(PACK)]
+
+        def leave(t):
+            nc.scalar.copy(a_sb[t][:], sums[t][0][:])
+            nc.vector.tensor_copy(b_sb[t][:], sums[t][1][:])
+
+        def put(t):
+            nc.scalar.activation(boards_w[t][:].indirect(idx3[:]), a_sb[t][:], ACT.Copy)
+            nc.vector.tensor_copy(boards_v[t][:].indirect(idx4[:]), b_sb[t][:])
+
+        def read(t):
+            nc.scalar.activation(read_w[t][:], boards_w[t][:].indirect(idx5[:]), ACT.Copy)
+            for h in range(O // P):
+                part = idx6[:, h * (P // 16) : (h + 1) * (P // 16)]
+                nc.vector.tensor_tensor(diffs[h][:, t, :], boards_v[t][:].indirect(part), read_w[t][:, halves[h]], ALU.subtract)
+
+        leave(0)
+        for t in range(PACK):
+            put(t)
+            if t + 1 < PACK:
+                leave(t + 1)
+            read(t)
+
+        for h in range(O // P):
+            hid = keep.tile([P, P, PACK], BF16, name="hid%d" % h, align_bytes=64)
+            nc.scalar.activation(hid[:], diffs[h][:].rearrange("p t o -> p o t"), ACT.Abs)
+            hid_w = keep.tile([P, P], U32, name="hid_w%d" % h, align_bytes=64)
+            hid_s = keep.tile([P, P], U8, name="hid_s%d" % h, align_bytes=64)
+            nc.vector.quantize_mx(out=hid_w[:].bitcast(E5M2), scales=hid_s[:], in_=hid[:].rearrange("p o t -> p (o t)"))
+            y_ps = psum.tile([P, N // P, P], F32, tag="bank", name="y_ps")
+            for g in range(N // P):
+                product(y_ps[:, g, :], (wb_w, wb_s, E4M3), slice(g * P, (g + 1) * P), (hid_w, hid_s, E5M2), True, True)
+            y_sb = keep.tile([P, N // P, P], F32, name="y_sb%d" % h)
+            nc.vector.tensor_copy(y_sb[:], y_ps[:])
+            nc.sync.dma_start(out[:, halves[h]].rearrange("(g p) o -> p g o", p=P), y_sb[:])

@@ -41,39 +41,47 @@ def tile_list_crossed_twoboards_one_plain_kernel(
             queue.dma_start(tile[:].bitcast(I32), src.bitcast(I32))
             return tile
 
-        def load_plane(name, src, cols, queue):
+        def cleared_plane(name, cols, engine):
             tile = keep.tile([P, cols], U8, name=name, align_bytes=64)
-            nc.vector.memset(tile[:].bitcast(I32), 0)
-            rows = src[0].bitcast(I32)
-            for q in range(4):
-                queue.dma_start(tile[32 * q : 32 * q + 4, :].bitcast(I32), rows[4 * q : 4 * q + 4, :])
+            engine.memset(tile[:].bitcast(I32), 0)
             return tile
+
+        def load_rows(plane, src, quadrants):
+            rows = src[0].bitcast(I32)
+            for q in quadrants:
+                nc.sync.dma_start(plane[32 * q : 32 * q + 4, :].bitcast(I32), rows[4 * q : 4 * q + 4, :])
 
         def flat(words):
             return words[0].rearrange("p c t -> p (c t)")
 
+        xt_s = cleared_plane("xt_s", T, nc.gpsimd)
+        xo_s = cleared_plane("xo_s", Z, nc.gpsimd)
+        ww_s = cleared_plane("ww_s", 2 * R, nc.gpsimd)
+        wb_s = cleared_plane("wb_s", N, nc.gpsimd)
         idx = load_list("idx", offs)
         xt_w = load_words("xt_w", xt_words[0], T, U16, nc.sync)
+        load_rows(xt_s, xt_scales, range(4))
         idx2 = load_list("idx2", offs2)
         xo_w = load_words("xo_w", flat(xo_words), Z, U32, nc.sync)
-        xt_s = load_plane("xt_s", xt_scales, T, nc.sync)
+        load_rows(xo_s, xo_scales, range(4))
+        load_rows(ww_s[:, :R], w_scales, range(2))
         w_w = load_words("w_w", flat(w_words), R, U32, nc.sync)
         w2_w = load_words("w2_w", flat(w2_words), R, U32, nc.sync)
-        xo_s = load_plane("xo_s", xo_scales, Z, nc.sync)
-        w_s = load_plane("w_s", w_scales, R, nc.sync)
-        w2_s = load_plane("w2_s", w2_scales, R, nc.sync)
+        load_rows(ww_s[:, :R], w_scales, range(2, 4))
+        load_rows(ww_s[:, R:], w2_scales, range(4))
         idx3 = load_list("idx3", offs3)
         idx4 = load_list("idx4", offs4)
         idx5 = load_list("idx5", offs5)
         idx6 = load_list("idx6", offs6)
         wb_w = load_words("wb_w", flat(wb_words), N, U32, nc.sync)
-        wb_s = load_plane("wb_s", wb_scales, N, nc.sync)
+        load_rows(wb_s, wb_scales, range(4))
 
         boards_w = [keep.tile([P, C], F32, name="pw%d" % t) for t in range(PACK)]
         boards_v = [keep.tile([P, C], F32, name="pv%d" % t) for t in range(PACK)]
         for t in range(PACK):
-            nc.vector.memset(boards_w[t][:], 0.0)
-            nc.vector.memset(boards_v[t][:], 0.0)
+            engine = nc.gpsimd
+            engine.memset(boards_v[t][:], 0.0)
+            engine.memset(boards_w[t][:], 0.0)
 
         def pick(name, window, offsets, dtype):
             tile = keep.tile([P, J], dtype, name=name, align_bytes=64)
@@ -85,51 +93,54 @@ def tile_list_crossed_twoboards_one_plain_kernel(
         xo_wg = pick("xo_wg", xo_w, idx2, U32)
         xo_sg = pick("xo_sg", xo_s, idx2, U8)
 
-        def deal(name, src, dtype, run, copy):
-            tile = keep.tile([P, R], dtype, name=name, align_bytes=64)
-            copy(
-                tile[:].rearrange("p (t c i) -> p c t i", t=PACK, i=run),
-                src[:].rearrange("p (c i t) -> p c t i", t=PACK, i=run),
+        def deal_words(name, src):
+            head = keep.tile([P, P], U32, name=name + "_head", align_bytes=64)
+            nc.scalar.copy(head[:], src[:].rearrange("p (m t) -> p t m", t=PACK)[:, 0, :])
+            rest = keep.tile([P, PACK - 1, P], U32, name=name + "_rest", align_bytes=64)
+            nc.scalar.copy(
+                rest[:].rearrange("p t (c i) -> p c t i", i=4),
+                src[:].rearrange("p (c i t) -> p c t i", t=PACK, i=4)[:, :, 1:, :],
             )
-            return tile
+            return [head[:]] + [rest[:, t, :] for t in range(PACK - 1)]
 
-        w_wd = deal("w_wd", w_w, U32, 4, nc.scalar.copy)
-        w_sd = deal("w_sd", w_s, U8, 16, nc.vector.tensor_copy)
-        w2_wd = deal("w2_wd", w2_w, U32, 4, nc.scalar.copy)
-        w2_sd = deal("w2_sd", w2_s, U8, 16, nc.vector.tensor_copy)
+        w_wd = deal_words("w_wd", w_w)
+        w2_wd = deal_words("w2_wd", w2_w)
+        head = keep.tile([P, 2 * P], U8, name="head", align_bytes=64)
+        nc.vector.tensor_copy(head[:], ww_s[:].rearrange("p (m t) -> p t m", t=PACK)[:, 0, :])
+        rest = keep.tile([P, PACK - 1, 2 * P], U8, name="rest", align_bytes=64)
+        nc.vector.tensor_copy(
+            rest[:].rearrange("p t (c i) -> p c t i", i=16),
+            ww_s[:].rearrange("p (c i t) -> p c t i", t=PACK, i=16)[:, :, 1:, :],
+        )
+        dealt = [head[:]] + [rest[:, t, :] for t in range(PACK - 1)]
+        w_sd = [plane[:, :P] for plane in dealt]
+        w2_sd = [plane[:, P:] for plane in dealt]
 
-        first = (w_wd, w_sd, E5M2)
-        second = (w2_wd, w2_sd, E4M3)
-        tokens = (xt_wg, xt_sg, E2M1)
-        notes = (xo_wg, xo_sg, E5M2)
+        tokens = (xt_wg[:].bitcast(E2M1), xt_sg[:])
+        notes = (xo_wg[:].bitcast(E5M2), xo_sg[:])
 
-        def product(acc, weight, cols, moving, start, stop):
+        def product(acc, weight, moving, start, stop):
             nc.tensor.matmul_mx(
-                out=acc,
-                lhsT=weight[0][:, cols].bitcast(weight[2]),
-                lhsT_scale=weight[1][:, cols],
-                rhs=moving[0][:].bitcast(moving[2]),
-                rhs_scale=moving[1][:],
-                start=start,
-                stop=stop,
+                out=acc, lhsT=weight[0], lhsT_scale=weight[1], rhs=moving[0], rhs_scale=moving[1], start=start, stop=stop
             )
 
         sums = []
         for t in range(PACK):
-            cols = slice(t * P, (t + 1) * P)
+            first = (w_wd[t].bitcast(E5M2), w_sd[t])
+            second = (w2_wd[t].bitcast(E4M3), w2_sd[t])
             a_ps = psum.tile([P, J], F32, tag="bank", name="a_ps")
-            product(a_ps[:], first, cols, tokens, True, False)
-            product(a_ps[:], second, cols, notes, False, True)
+            product(a_ps[:], first, tokens, True, False)
+            product(a_ps[:], second, notes, False, True)
             b_ps = psum.tile([P, J], F32, tag="bank", name="b_ps")
-            product(b_ps[:], second, cols, tokens, True, False)
-            product(b_ps[:], first, cols, notes, False, True)
+            product(b_ps[:], second, tokens, True, False)
+            product(b_ps[:], first, notes, False, True)
             sums.append((a_ps, b_ps))
 
         halves = [slice(h * P, (h + 1) * P) for h in range(O // P)]
         diffs = [keep.tile([P, PACK, P], F32, name="diff%d" % h) for h in range(O // P)]
         a_sb = [keep.tile([P, J], F32, name="a_sb%d" % t) for t in range(PACK)]
         b_sb = [keep.tile([P, J], F32, name="b_sb%d" % t) for t in range(PACK)]
-        read_w = [keep.tile([P, O], F32, name="read_w%d" % t) for t in range(PACK)]
+        read_w = [keep.tile([P, PACK, P], F32, name="read_w%d" % h) for h in range(O // P)]
 
         def leave(t):
             nc.scalar.copy(a_sb[t][:], sums[t][0][:])
@@ -139,28 +150,36 @@ def tile_list_crossed_twoboards_one_plain_kernel(
             nc.scalar.activation(boards_w[t][:].indirect(idx3[:]), a_sb[t][:], ACT.Copy)
             nc.vector.tensor_copy(boards_v[t][:].indirect(idx4[:]), b_sb[t][:])
 
-        def read(t):
-            nc.scalar.activation(read_w[t][:], boards_w[t][:].indirect(idx5[:]), ACT.Copy)
-            for h in range(O // P):
-                part = idx6[:, h * (P // 16) : (h + 1) * (P // 16)]
-                nc.vector.tensor_tensor(diffs[h][:, t, :], boards_v[t][:].indirect(part), read_w[t][:, halves[h]], ALU.subtract)
+        def read(t, h):
+            part = slice(h * (P // 16), (h + 1) * (P // 16))
+            nc.scalar.activation(read_w[h][:, t, :], boards_w[t][:].indirect(idx5[:, part]), ACT.Copy)
+            nc.vector.tensor_tensor(diffs[h][:, t, :], boards_v[t][:].indirect(idx6[:, part]), read_w[h][:, t, :], ALU.subtract)
 
-        leave(0)
         for t in range(PACK):
+            leave(t)
             put(t)
-            if t + 1 < PACK:
-                leave(t + 1)
-            read(t)
+        for h in range(O // P):
+            for t in range(PACK):
+                read(t, h)
 
         for h in range(O // P):
             hid = keep.tile([P, P, PACK], BF16, name="hid%d" % h, align_bytes=64)
-            nc.scalar.activation(hid[:], diffs[h][:].rearrange("p t o -> p o t"), ACT.Abs)
+            turned = diffs[h][:].rearrange("p t o -> p o t")
+            share = P if h == 0 else P // 2
+            nc.scalar.activation(hid[:, :share, :], turned[:, :share, :], ACT.Abs)
+            if share < P:
+                nc.vector.scalar_tensor_tensor(hid[:, share:, :], turned[:, share:, :], -1.0, turned[:, share:, :], ALU.mult, ALU.max)
             hid_w = keep.tile([P, P], U32, name="hid_w%d" % h, align_bytes=64)
             hid_s = keep.tile([P, P], U8, name="hid_s%d" % h, align_bytes=64)
             nc.vector.quantize_mx(out=hid_w[:].bitcast(E5M2), scales=hid_s[:], in_=hid[:].rearrange("p o t -> p (o t)"))
-            y_ps = psum.tile([P, N // P, P], F32, tag="bank", name="y_ps")
             for g in range(N // P):
-                product(y_ps[:, g, :], (wb_w, wb_s, E4M3), slice(g * P, (g + 1) * P), (hid_w, hid_s, E5M2), True, True)
-            y_sb = keep.tile([P, N // P, P], F32, name="y_sb%d" % h)
-            nc.vector.tensor_copy(y_sb[:], y_ps[:])
-            nc.sync.dma_start(out[:, halves[h]].rearrange("(g p) o -> p g o", p=P), y_sb[:])
+                rows = slice(g * P, (g + 1) * P)
+                y_ps = psum.tile([P, P], F32, tag="bank", name="y_ps")
+                product(y_ps[:], (wb_w[:, rows].bitcast(E4M3), wb_s[:, rows]), (hid_w[:].bitcast(E5M2), hid_s[:]), True, True)
+                y_sb = keep.tile([P, P], F32, name="y_sb%d%d" % (h, g))
+                if g == 0:
+                    nc.scalar.copy(y_sb[:], y_ps[:])
+                    nc.scalar.dma_start(out[rows, halves[h]], y_sb[:])
+                else:
+                    nc.vector.tensor_copy(y_sb[:], y_ps[:])
+                    nc.sync.dma_start(out[rows, halves[h]], y_sb[:])

@@ -19,6 +19,14 @@ ALU = mybir.AluOpType
 
 P = 128
 PACK = 4
+QUADRANTS = 4
+PER_COLUMN = 16
+BANKS = 8
+HALF = O // 2
+WORD_RUN = 4
+BYTE_RUN = 16
+A_SLICE_ON_VECTOR = 1
+ABS_ON_SCALAR = (HALF, HALF // 2)
 
 
 def tile_list_crossed_twoboards_one_plain_kernel(
@@ -29,21 +37,21 @@ def tile_list_crossed_twoboards_one_plain_kernel(
     with ExitStack() as ctx:
         lists = ctx.enter_context(tc.tile_pool(name="lists", bufs=1))
         keep = ctx.enter_context(tc.tile_pool(name="keep", bufs=1))
-        psum = ctx.enter_context(tc.psum_pool(name="psum", bufs=8))
+        psum = ctx.enter_context(tc.psum_pool(name="psum", bufs=BANKS))
 
         def load_list(name, src):
-            tile = lists.tile([P, J // 16], U16, name=name)
+            tile = lists.tile([P, J // PER_COLUMN], U16, name=name)
             nc.sync.dma_start(tile[:], src)
             return tile
 
-        def load_words(name, src, cols, dtype, queue):
+        def load_words(name, src, cols, dtype):
             tile = keep.tile([P, cols], dtype, name=name, align_bytes=64)
-            queue.dma_start(tile[:].bitcast(I32), src.bitcast(I32))
+            nc.sync.dma_start(tile[:].bitcast(I32), src.bitcast(I32))
             return tile
 
-        def cleared_plane(name, cols, engine):
+        def cleared_plane(name, cols):
             tile = keep.tile([P, cols], U8, name=name, align_bytes=64)
-            engine.memset(tile[:].bitcast(I32), 0)
+            nc.gpsimd.memset(tile[:].bitcast(I32), 0)
             return tile
 
         def load_rows(plane, src, quadrants):
@@ -54,34 +62,34 @@ def tile_list_crossed_twoboards_one_plain_kernel(
         def flat(words):
             return words[0].rearrange("p c t -> p (c t)")
 
-        xt_s = cleared_plane("xt_s", T, nc.gpsimd)
-        xo_s = cleared_plane("xo_s", Z, nc.gpsimd)
-        ww_s = cleared_plane("ww_s", 2 * R, nc.gpsimd)
-        wb_s = cleared_plane("wb_s", N, nc.gpsimd)
+        xt_s = cleared_plane("xt_s", T)
+        xo_s = cleared_plane("xo_s", Z)
+        ww_s = cleared_plane("ww_s", 2 * R)
+        wb_s = cleared_plane("wb_s", N)
+
         idx = load_list("idx", offs)
-        xt_w = load_words("xt_w", xt_words[0], T, U16, nc.sync)
-        load_rows(xt_s, xt_scales, range(4))
+        xt_w = load_words("xt_w", xt_words[0], T, U16)
+        load_rows(xt_s, xt_scales, range(QUADRANTS))
         idx2 = load_list("idx2", offs2)
-        xo_w = load_words("xo_w", flat(xo_words), Z, U32, nc.sync)
-        load_rows(xo_s, xo_scales, range(4))
-        load_rows(ww_s[:, :R], w_scales, range(2))
-        w_w = load_words("w_w", flat(w_words), R, U32, nc.sync)
-        w2_w = load_words("w2_w", flat(w2_words), R, U32, nc.sync)
-        load_rows(ww_s[:, :R], w_scales, range(2, 4))
-        load_rows(ww_s[:, R:], w2_scales, range(4))
+        xo_w = load_words("xo_w", flat(xo_words), Z, U32)
+        load_rows(xo_s, xo_scales, range(QUADRANTS))
+        load_rows(ww_s[:, :R], w_scales, range(QUADRANTS // 2))
+        w_w = load_words("w_w", flat(w_words), R, U32)
+        w2_w = load_words("w2_w", flat(w2_words), R, U32)
+        load_rows(ww_s[:, :R], w_scales, range(QUADRANTS // 2, QUADRANTS))
+        load_rows(ww_s[:, R:], w2_scales, range(QUADRANTS))
         idx3 = load_list("idx3", offs3)
         idx4 = load_list("idx4", offs4)
         idx5 = load_list("idx5", offs5)
         idx6 = load_list("idx6", offs6)
-        wb_w = load_words("wb_w", flat(wb_words), N, U32, nc.sync)
-        load_rows(wb_s, wb_scales, range(4))
+        wb_w = load_words("wb_w", flat(wb_words), N, U32)
+        load_rows(wb_s, wb_scales, range(QUADRANTS))
 
-        boards_w = [keep.tile([P, C], F32, name="pw%d" % t) for t in range(PACK)]
-        boards_v = [keep.tile([P, C], F32, name="pv%d" % t) for t in range(PACK)]
+        pw = [keep.tile([P, C], F32, name="pw%d" % t) for t in range(PACK)]
+        pv = [keep.tile([P, C], F32, name="pv%d" % t) for t in range(PACK)]
         for t in range(PACK):
-            engine = nc.gpsimd
-            engine.memset(boards_v[t][:], 0.0)
-            engine.memset(boards_w[t][:], 0.0)
+            nc.gpsimd.memset(pv[t][:], 0.0)
+            nc.gpsimd.memset(pw[t][:], 0.0)
 
         def pick(name, window, offsets, dtype):
             tile = keep.tile([P, J], dtype, name=name, align_bytes=64)
@@ -98,23 +106,27 @@ def tile_list_crossed_twoboards_one_plain_kernel(
             nc.scalar.copy(head[:], src[:].rearrange("p (m t) -> p t m", t=PACK)[:, 0, :])
             rest = keep.tile([P, PACK - 1, P], U32, name=name + "_rest", align_bytes=64)
             nc.scalar.copy(
-                rest[:].rearrange("p t (c i) -> p c t i", i=4),
-                src[:].rearrange("p (c i t) -> p c t i", t=PACK, i=4)[:, :, 1:, :],
+                rest[:].rearrange("p t (c i) -> p c t i", i=WORD_RUN),
+                src[:].rearrange("p (c i t) -> p c t i", t=PACK, i=WORD_RUN)[:, :, 1:, :],
             )
             return [head[:]] + [rest[:, t, :] for t in range(PACK - 1)]
 
+        def deal_first_bytes(name, src):
+            head = keep.tile([P, P], U8, name=name, align_bytes=64)
+            nc.vector.tensor_copy(head[:], src.rearrange("p (m t) -> p t m", t=PACK)[:, 0, :])
+            return head[:]
+
         w_wd = deal_words("w_wd", w_w)
         w2_wd = deal_words("w2_wd", w2_w)
-        head = keep.tile([P, 2 * P], U8, name="head", align_bytes=64)
-        nc.vector.tensor_copy(head[:], ww_s[:].rearrange("p (m t) -> p t m", t=PACK)[:, 0, :])
-        rest = keep.tile([P, PACK - 1, 2 * P], U8, name="rest", align_bytes=64)
+        w_s0 = deal_first_bytes("w_s0", ww_s[:, :R])
+        w2_s0 = deal_first_bytes("w2_s0", ww_s[:, R:])
+        ww_sd = keep.tile([P, PACK - 1, 2 * P], U8, name="ww_sd", align_bytes=64)
         nc.vector.tensor_copy(
-            rest[:].rearrange("p t (c i) -> p c t i", i=16),
-            ww_s[:].rearrange("p (c i t) -> p c t i", t=PACK, i=16)[:, :, 1:, :],
+            ww_sd[:].rearrange("p t (c i) -> p c t i", i=BYTE_RUN),
+            ww_s[:].rearrange("p (c i t) -> p c t i", t=PACK, i=BYTE_RUN)[:, :, 1:, :],
         )
-        dealt = [head[:]] + [rest[:, t, :] for t in range(PACK - 1)]
-        w_sd = [plane[:, :P] for plane in dealt]
-        w2_sd = [plane[:, P:] for plane in dealt]
+        w_sd = [w_s0] + [ww_sd[:, t, :P] for t in range(PACK - 1)]
+        w2_sd = [w2_s0] + [ww_sd[:, t, P:] for t in range(PACK - 1)]
 
         tokens = (xt_wg[:].bitcast(E2M1), xt_sg[:])
         notes = (xo_wg[:].bitcast(E5M2), xo_sg[:])
@@ -124,62 +136,67 @@ def tile_list_crossed_twoboards_one_plain_kernel(
                 out=acc, lhsT=weight[0], lhsT_scale=weight[1], rhs=moving[0], rhs_scale=moving[1], start=start, stop=stop
             )
 
-        sums = []
+        a_ps, b_ps = [], []
         for t in range(PACK):
             first = (w_wd[t].bitcast(E5M2), w_sd[t])
             second = (w2_wd[t].bitcast(E4M3), w2_sd[t])
-            a_ps = psum.tile([P, J], F32, tag="bank", name="a_ps")
-            product(a_ps[:], first, tokens, True, False)
-            product(a_ps[:], second, notes, False, True)
-            b_ps = psum.tile([P, J], F32, tag="bank", name="b_ps")
-            product(b_ps[:], second, tokens, True, False)
-            product(b_ps[:], first, notes, False, True)
-            sums.append((a_ps, b_ps))
+            a_ps.append(psum.tile([P, J], F32, tag="bank", name="a_ps"))
+            b_ps.append(psum.tile([P, J], F32, tag="bank", name="b_ps"))
+            if t == 0:
+                product(a_ps[t][:], first, tokens, True, False)
+                product(b_ps[t][:], first, notes, True, False)
+                product(a_ps[t][:], second, notes, False, True)
+                product(b_ps[t][:], second, tokens, False, True)
+            else:
+                product(a_ps[t][:], first, tokens, True, False)
+                product(a_ps[t][:], second, notes, False, True)
+                product(b_ps[t][:], second, tokens, True, False)
+                product(b_ps[t][:], first, notes, False, True)
 
-        halves = [slice(h * P, (h + 1) * P) for h in range(O // P)]
-        diffs = [keep.tile([P, PACK, P], F32, name="diff%d" % h) for h in range(O // P)]
+        halves = [slice(0, HALF), slice(HALF, O)]
+        diff = [keep.tile([P, PACK, HALF], F32, name="diff%d" % h) for h in range(len(halves))]
         a_sb = [keep.tile([P, J], F32, name="a_sb%d" % t) for t in range(PACK)]
         b_sb = [keep.tile([P, J], F32, name="b_sb%d" % t) for t in range(PACK)]
-        read_w = [keep.tile([P, PACK, P], F32, name="read_w%d" % h) for h in range(O // P)]
-
-        def leave(t):
-            nc.scalar.copy(a_sb[t][:], sums[t][0][:])
-            nc.vector.tensor_copy(b_sb[t][:], sums[t][1][:])
-
-        def put(t):
-            nc.scalar.activation(boards_w[t][:].indirect(idx3[:]), a_sb[t][:], ACT.Copy)
-            nc.vector.tensor_copy(boards_v[t][:].indirect(idx4[:]), b_sb[t][:])
-
-        def read(t, h):
-            part = slice(h * (P // 16), (h + 1) * (P // 16))
-            nc.scalar.activation(read_w[h][:, t, :], boards_w[t][:].indirect(idx5[:, part]), ACT.Copy)
-            nc.vector.tensor_tensor(diffs[h][:, t, :], boards_v[t][:].indirect(idx6[:, part]), read_w[h][:, t, :], ALU.subtract)
+        pw_read = [keep.tile([P, PACK, HALF], F32, name="pw_read%d" % h) for h in range(len(halves))]
 
         for t in range(PACK):
-            leave(t)
-            put(t)
-        for h in range(O // P):
-            for t in range(PACK):
-                read(t, h)
+            if t == A_SLICE_ON_VECTOR:
+                nc.vector.tensor_copy(a_sb[t][:], a_ps[t][:])
+            else:
+                nc.scalar.copy(a_sb[t][:], a_ps[t][:])
+            nc.vector.tensor_copy(b_sb[t][:], b_ps[t][:])
+            nc.scalar.activation(pw[t][:].indirect(idx3[:]), a_sb[t][:], ACT.Copy)
+            nc.vector.tensor_copy(pv[t][:].indirect(idx4[:]), b_sb[t][:])
 
-        for h in range(O // P):
-            hid = keep.tile([P, P, PACK], BF16, name="hid%d" % h, align_bytes=64)
-            turned = diffs[h][:].rearrange("p t o -> p o t")
-            share = P if h == 0 else P // 2
+        for h, half in enumerate(halves):
+            entries = slice(half.start // PER_COLUMN, half.stop // PER_COLUMN)
+            for t in range(PACK):
+                nc.scalar.activation(pw_read[h][:, t, :], pw[t][:].indirect(idx5[:, entries]), ACT.Copy)
+                nc.vector.tensor_tensor(
+                    diff[h][:, t, :], pv[t][:].indirect(idx6[:, entries]), pw_read[h][:, t, :], ALU.subtract
+                )
+
+        for h, half in enumerate(halves):
+            hid = keep.tile([P, HALF, PACK], BF16, name="hid%d" % h, align_bytes=64)
+            turned = diff[h][:].rearrange("p t o -> p o t")
+            share = ABS_ON_SCALAR[h]
             nc.scalar.activation(hid[:, :share, :], turned[:, :share, :], ACT.Abs)
-            if share < P:
-                nc.vector.scalar_tensor_tensor(hid[:, share:, :], turned[:, share:, :], -1.0, turned[:, share:, :], ALU.mult, ALU.max)
-            hid_w = keep.tile([P, P], U32, name="hid_w%d" % h, align_bytes=64)
-            hid_s = keep.tile([P, P], U8, name="hid_s%d" % h, align_bytes=64)
+            if share < HALF:
+                nc.vector.scalar_tensor_tensor(
+                    hid[:, share:, :], turned[:, share:, :], -1.0, turned[:, share:, :], ALU.mult, ALU.max
+                )
+            hid_w = keep.tile([P, HALF], U32, name="hid_w%d" % h, align_bytes=64)
+            hid_s = keep.tile([P, HALF], U8, name="hid_s%d" % h, align_bytes=64)
             nc.vector.quantize_mx(out=hid_w[:].bitcast(E5M2), scales=hid_s[:], in_=hid[:].rearrange("p o t -> p (o t)"))
+
             for g in range(N // P):
                 rows = slice(g * P, (g + 1) * P)
-                y_ps = psum.tile([P, P], F32, tag="bank", name="y_ps")
+                y_ps = psum.tile([P, HALF], F32, tag="bank", name="y_ps")
                 product(y_ps[:], (wb_w[:, rows].bitcast(E4M3), wb_s[:, rows]), (hid_w[:].bitcast(E5M2), hid_s[:]), True, True)
-                y_sb = keep.tile([P, P], F32, name="y_sb%d%d" % (h, g))
+                y_sb = keep.tile([P, HALF], F32, name="y_sb%d%d" % (h, g))
                 if g == 0:
                     nc.scalar.copy(y_sb[:], y_ps[:])
-                    nc.scalar.dma_start(out[rows, halves[h]], y_sb[:])
+                    nc.scalar.dma_start(out[rows, half], y_sb[:])
                 else:
                     nc.vector.tensor_copy(y_sb[:], y_ps[:])
-                    nc.sync.dma_start(out[rows, halves[h]], y_sb[:])
+                    nc.sync.dma_start(out[rows, half], y_sb[:])

@@ -25,7 +25,7 @@ BANKS = 8
 HALF = O // 2
 WORD_RUN = 4
 BYTE_RUN = 16
-A_SLICE_ON_VECTOR = 1
+B_SLICE_ON_SCALAR = 2
 ABS_ON_SCALAR = (HALF, HALF // 2)
 
 
@@ -160,11 +160,11 @@ def tile_list_crossed_twoboards_one_plain_kernel(
         pw_read = [keep.tile([P, PACK, HALF], F32, name="pw_read%d" % h) for h in range(len(halves))]
 
         for t in range(PACK):
-            if t == A_SLICE_ON_VECTOR:
-                nc.vector.tensor_copy(a_sb[t][:], a_ps[t][:])
+            nc.scalar.copy(a_sb[t][:], a_ps[t][:])
+            if t == B_SLICE_ON_SCALAR:
+                nc.scalar.copy(b_sb[t][:], b_ps[t][:])
             else:
-                nc.scalar.copy(a_sb[t][:], a_ps[t][:])
-            nc.vector.tensor_copy(b_sb[t][:], b_ps[t][:])
+                nc.vector.tensor_copy(b_sb[t][:], b_ps[t][:])
             nc.scalar.activation(pw[t][:].indirect(idx3[:]), a_sb[t][:], ACT.Copy)
             nc.vector.tensor_copy(pv[t][:].indirect(idx4[:]), b_sb[t][:])
 

from contextlib import ExitStack

import concourse.mybir as mybir

K, T, Z, J, R, C, O, N = 512, 1024, 1024, 256, 512, 512, 256, 256
FLOPS = 2 * (4 * K * R * J + R * N * O)

F32 = mybir.dt.float32
BF16 = mybir.dt.bfloat16
I32 = mybir.dt.int32
U32 = mybir.dt.uint32
U16 = mybir.dt.uint16
U8 = mybir.dt.uint8
E4M3 = mybir.dt.float8_e4m3fn_x4
E5M2 = mybir.dt.float8_e5m2_x4
E2M1 = mybir.dt.float4_e2m1fn_x4
ACT = mybir.ActivationFunctionType
ALU = mybir.AluOpType

P = 128
PACK = 4
QUADRANTS = 4
PER_COLUMN = 16
BANKS = 8
HALF = O // 2
WORD_RUN = 4
BYTE_RUN = 16
B_SLICE_ON_SCALAR = 2
ABS_ON_SCALAR = (HALF, HALF // 2)


def tile_list_crossed_twoboards_one_plain_kernel(
    tc, xt_words, xt_scales, xo_words, xo_scales, w_words, w_scales, w2_words, w2_scales,
    wb_words, wb_scales, offs, offs2, offs3, offs4, offs5, offs6, out,
):
    nc = tc.nc
    with ExitStack() as ctx:
        lists = ctx.enter_context(tc.tile_pool(name="lists", bufs=1))
        keep = ctx.enter_context(tc.tile_pool(name="keep", bufs=1))
        psum = ctx.enter_context(tc.psum_pool(name="psum", bufs=BANKS))

        def load_list(name, src):
            tile = lists.tile([P, J // PER_COLUMN], U16, name=name)
            nc.sync.dma_start(tile[:], src)
            return tile

        def load_words(name, src, cols, dtype):
            tile = keep.tile([P, cols], dtype, name=name, align_bytes=64)
            nc.sync.dma_start(tile[:].bitcast(I32), src.bitcast(I32))
            return tile

        def cleared_plane(name, cols):
            tile = keep.tile([P, cols], U8, name=name, align_bytes=64)
            nc.gpsimd.memset(tile[:].bitcast(I32), 0)
            return tile

        def load_rows(plane, src, quadrants):
            rows = src[0].bitcast(I32)
            for q in quadrants:
                nc.sync.dma_start(plane[32 * q : 32 * q + 4, :].bitcast(I32), rows[4 * q : 4 * q + 4, :])

        def flat(words):
            return words[0].rearrange("p c t -> p (c t)")

        xt_s = cleared_plane("xt_s", T)
        xo_s = cleared_plane("xo_s", Z)
        ww_s = cleared_plane("ww_s", 2 * R)
        wb_s = cleared_plane("wb_s", N)

        idx = load_list("idx", offs)
        xt_w = load_words("xt_w", xt_words[0], T, U16)
        load_rows(xt_s, xt_scales, range(QUADRANTS))
        idx2 = load_list("idx2", offs2)
        xo_w = load_words("xo_w", flat(xo_words), Z, U32)
        load_rows(xo_s, xo_scales, range(QUADRANTS))
        load_rows(ww_s[:, :R], w_scales, range(QUADRANTS // 2))
        w_w = load_words("w_w", flat(w_words), R, U32)
        w2_w = load_words("w2_w", flat(w2_words), R, U32)
        load_rows(ww_s[:, :R], w_scales, range(QUADRANTS // 2, QUADRANTS))
        load_rows(ww_s[:, R:], w2_scales, range(QUADRANTS))
        idx3 = load_list("idx3", offs3)
        idx4 = load_list("idx4", offs4)
        idx5 = load_list("idx5", offs5)
        idx6 = load_list("idx6", offs6)
        wb_w = load_words("wb_w", flat(wb_words), N, U32)
        load_rows(wb_s, wb_scales, range(QUADRANTS))

        pw = [keep.tile([P, C], F32, name="pw%d" % t) for t in range(PACK)]
        pv = [keep.tile([P, C], F32, name="pv%d" % t) for t in range(PACK)]
        for t in range(PACK):
            nc.gpsimd.memset(pv[t][:], 0.0)
            nc.gpsimd.memset(pw[t][:], 0.0)

        def pick(name, window, offsets, dtype):
            tile = keep.tile([P, J], dtype, name=name, align_bytes=64)
            nc.vector.tensor_copy(tile[:], window[:].indirect(offsets[:]))
            return tile

        xt_wg = pick("xt_wg", xt_w, idx, U16)
        xt_sg = pick("xt_sg", xt_s, idx, U8)
        xo_wg = pick("xo_wg", xo_w, idx2, U32)
        xo_sg = pick("xo_sg", xo_s, idx2, U8)

        def deal_words(name, src):
            head = keep.tile([P, P], U32, name=name + "_head", align_bytes=64)
            nc.scalar.copy(head[:], src[:].rearrange("p (m t) -> p t m", t=PACK)[:, 0, :])
            rest = keep.tile([P, PACK - 1, P], U32, name=name + "_rest", align_bytes=64)
            nc.scalar.copy(
                rest[:].rearrange("p t (c i) -> p c t i", i=WORD_RUN),
                src[:].rearrange("p (c i t) -> p c t i", t=PACK, i=WORD_RUN)[:, :, 1:, :],
            )
            return [head[:]] + [rest[:, t, :] for t in range(PACK - 1)]

        def deal_first_bytes(name, src):
            head = keep.tile([P, P], U8, name=name, align_bytes=64)
            nc.vector.tensor_copy(head[:], src.rearrange("p (m t) -> p t m", t=PACK)[:, 0, :])
            return head[:]

        w_wd = deal_words("w_wd", w_w)
        w2_wd = deal_words("w2_wd", w2_w)
        w_s0 = deal_first_bytes("w_s0", ww_s[:, :R])
        w2_s0 = deal_first_bytes("w2_s0", ww_s[:, R:])
        ww_sd = keep.tile([P, PACK - 1, 2 * P], U8, name="ww_sd", align_bytes=64)
        nc.vector.tensor_copy(
            ww_sd[:].rearrange("p t (c i) -> p c t i", i=BYTE_RUN),
            ww_s[:].rearrange("p (c i t) -> p c t i", t=PACK, i=BYTE_RUN)[:, :, 1:, :],
        )
        w_sd = [w_s0] + [ww_sd[:, t, :P] for t in range(PACK - 1)]
        w2_sd = [w2_s0] + [ww_sd[:, t, P:] for t in range(PACK - 1)]

        tokens = (xt_wg[:].bitcast(E2M1), xt_sg[:])
        notes = (xo_wg[:].bitcast(E5M2), xo_sg[:])

        def product(acc, weight, moving, start, stop):
            nc.tensor.matmul_mx(
                out=acc, lhsT=weight[0], lhsT_scale=weight[1], rhs=moving[0], rhs_scale=moving[1], start=start, stop=stop
            )

        a_ps, b_ps = [], []
        for t in range(PACK):
            first = (w_wd[t].bitcast(E5M2), w_sd[t])
            second = (w2_wd[t].bitcast(E4M3), w2_sd[t])
            a_ps.append(psum.tile([P, J], F32, tag="bank", name="a_ps"))
            b_ps.append(psum.tile([P, J], F32, tag="bank", name="b_ps"))
            if t == 0:
                product(a_ps[t][:], first, tokens, True, False)
                product(b_ps[t][:], first, notes, True, False)
                product(a_ps[t][:], second, notes, False, True)
                product(b_ps[t][:], second, tokens, False, True)
            else:
                product(a_ps[t][:], first, tokens, True, False)
                product(a_ps[t][:], second, notes, False, True)
                product(b_ps[t][:], second, tokens, True, False)
                product(b_ps[t][:], first, notes, False, True)

        halves = [slice(0, HALF), slice(HALF, O)]
        diff = [keep.tile([P, PACK, HALF], F32, name="diff%d" % h) for h in range(len(halves))]
        a_sb = [keep.tile([P, J], F32, name="a_sb%d" % t) for t in range(PACK)]
        b_sb = [keep.tile([P, J], F32, name="b_sb%d" % t) for t in range(PACK)]
        pw_read = [keep.tile([P, PACK, HALF], F32, name="pw_read%d" % h) for h in range(len(halves))]

        for t in range(PACK):
            nc.scalar.copy(a_sb[t][:], a_ps[t][:])
            if t == B_SLICE_ON_SCALAR:
                nc.scalar.copy(b_sb[t][:], b_ps[t][:])
            else:
                nc.vector.tensor_copy(b_sb[t][:], b_ps[t][:])
            nc.scalar.activation(pw[t][:].indirect(idx3[:]), a_sb[t][:], ACT.Copy)
            nc.vector.tensor_copy(pv[t][:].indirect(idx4[:]), b_sb[t][:])

        for h, half in enumerate(halves):
            entries = slice(half.start // PER_COLUMN, half.stop // PER_COLUMN)
            for t in range(PACK):
                nc.scalar.activation(pw_read[h][:, t, :], pw[t][:].indirect(idx5[:, entries]), ACT.Copy)
                nc.vector.tensor_tensor(
                    diff[h][:, t, :], pv[t][:].indirect(idx6[:, entries]), pw_read[h][:, t, :], ALU.subtract
                )

        for h, half in enumerate(halves):
            hid = keep.tile([P, HALF, PACK], BF16, name="hid%d" % h, align_bytes=64)
            turned = diff[h][:].rearrange("p t o -> p o t")
            share = ABS_ON_SCALAR[h]
            nc.scalar.activation(hid[:, :share, :], turned[:, :share, :], ACT.Abs)
            if share < HALF:
                nc.vector.scalar_tensor_tensor(
                    hid[:, share:, :], turned[:, share:, :], -1.0, turned[:, share:, :], ALU.mult, ALU.max
                )
            hid_w = keep.tile([P, HALF], U32, name="hid_w%d" % h, align_bytes=64)
            hid_s = keep.tile([P, HALF], U8, name="hid_s%d" % h, align_bytes=64)
            nc.vector.quantize_mx(out=hid_w[:].bitcast(E5M2), scales=hid_s[:], in_=hid[:].rearrange("p o t -> p (o t)"))

            for g in range(N // P):
                rows = slice(g * P, (g + 1) * P)
                y_ps = psum.tile([P, HALF], F32, tag="bank", name="y_ps")
                product(y_ps[:], (wb_w[:, rows].bitcast(E4M3), wb_s[:, rows]), (hid_w[:].bitcast(E5M2), hid_s[:]), True, True)
                y_sb = keep.tile([P, HALF], F32, name="y_sb%d%d" % (h, g))
                if g == 0:
                    nc.scalar.copy(y_sb[:], y_ps[:])
                    nc.scalar.dma_start(out[rows, half], y_sb[:])
                else:
                    nc.vector.tensor_copy(y_sb[:], y_ps[:])
                    nc.sync.dma_start(out[rows, half], y_sb[:])
